import numpy as np
import ml_dtypes


def mxq(x, axis, fmt="e4m3"):
    dtype, down = {"e4m3": (ml_dtypes.float8_e4m3fn, 7), "e5m2": (ml_dtypes.float8_e5m2, 14)}[fmt]
    v = np.moveaxis(np.asarray(x, np.float32).astype(ml_dtypes.bfloat16).astype(np.float64), axis, -1)
    blocks = v.reshape(v.shape[:-1] + (-1, 32))
    amax = np.abs(blocks).max(-1, keepdims=True)
    byte = np.maximum(np.where(amax > 0, np.frexp(amax)[1] - 1 + 127, 0) - down, 1)
    scale = np.exp2(byte - 127.0)
    codes = (blocks / scale).astype(np.float32).astype(dtype).astype(np.float64)
    return np.moveaxis((codes * scale).reshape(v.shape), -1, axis)


WIDE = False


def mx_kscale(k):
    if not WIDE:
        return np.ones(k)
    levels = np.array([10, -10, 5, -5, 0])
    if k % 512:
        return np.exp2(np.random.permutation(np.resize(levels, k // 32))).repeat(32)
    a = np.empty((k // 512, 16))
    for p in range(k // 512):
        a[p, :8] = np.random.permutation(np.resize(levels, 8))
        for g in range(8):
            far = levels[np.abs(levels - a[p, g]) >= 10]
            a[p, g + 8] = far[np.random.randint(len(far))]
    return np.exp2(a.ravel()).repeat(32)


BF16 = ml_dtypes.bfloat16


def bf(x):
    return np.asarray(x, np.float32).astype(BF16)


def f64(x):
    return np.asarray(x).astype(np.float64)


E2M1 = np.array([0.0, 0.5, 1.0, 1.5, 2.0, 3.0, 4.0, 6.0, -0.0, -0.5, -1.0, -1.5, -2.0, -3.0, -4.0, -6.0])


def pack_weight(w, fmt):
    k, n = w.shape
    w = f64(bf(w)).reshape(k // 32, 32, n)
    amax = np.abs(w).max(1)
    if fmt == "e4m3":
        byte = np.frexp(amax)[1] - 1 + 127 - 7
    else:
        mant, ex = np.frexp(amax / 6.0)
        byte = np.where(mant > 0.5, ex, ex - 1) + 127
    byte = np.clip(np.where(amax > 0, byte, 1), 1, 254)
    scaled = (w * np.exp2(127.0 - byte)[:, None, :]).reshape(k, n).astype(np.float32)
    by_word = np.ascontiguousarray(scaled.reshape(k // 512, 128, 4, n).transpose(0, 1, 3, 2))
    if fmt == "e4m3":
        words = by_word.astype(ml_dtypes.float8_e4m3fn).view(np.uint8)
    else:
        c = by_word.astype(ml_dtypes.float4_e2m1fn).view(np.uint8) & 0xF
        words = c[..., 0::2] | (c[..., 1::2] << 4)
    return np.ascontiguousarray(words), np.ascontiguousarray(byte.astype(np.uint8).reshape(k // 512, 16, n))


def unpack_weight(words, scales, fmt):
    g, p, n, _ = words.shape
    if fmt == "e4m3":
        vals = np.ascontiguousarray(words).view(ml_dtypes.float8_e4m3fn).astype(np.float64)
    else:
        nib = np.empty((g, p, n, 4), np.uint8)
        nib[..., 0::2] = words & 0xF
        nib[..., 1::2] = words >> 4
        vals = E2M1[nib]
    vals = vals * np.repeat(np.exp2(scales.astype(np.float64) - 127.0), 8, axis=1)[..., None]
    return vals.transpose(0, 1, 3, 2).reshape(g * 512, n)
def pack4(w):
    words, scales = pack_weight(w, "e2m1")
    return words.reshape(words.shape[0], 128, -1), scales


def unpack4(words, scales):
    return unpack_weight(words.reshape(words.shape[0], 128, -1, 2), scales, "e2m1")


T, DX, DZ, DG, E, L = 1024, 1024, 1024, 1024, 1024, 3


def modulator(z, gates, wh_words, wh_scales, bh):
    c = np.sum(f64(gates).T[:, :, None] * f64(z), axis=0)
    return (mxq(c, 1, "e4m3") @ unpack4(wh_words, wh_scales)) + f64(bh)[None, :]


def draw0():
    a, b, u = mx_kscale(DZ), mx_kscale(DG), mx_kscale(T)
    x = bf(np.random.standard_normal((T, DX)) * u[:, None])
    z = bf(np.random.standard_normal((L, T, DZ)) * a)
    gates = bf(np.random.standard_normal((T, L)) * 0.6)
    wh_words, wh_scales = pack4(np.random.standard_normal((DZ, E)) / np.sqrt(DZ) / a[:, None])
    bh = bf(np.random.standard_normal(E) * 0.4)
    wp_words, wp_scales = pack4((np.random.standard_normal((E, DG)) / np.sqrt(DG) / b[None, :]).T)
    g = bf(np.random.standard_normal((T, DG)) * b[None, :] / u[:, None])
    return {
        "x": x,
        "z": z,
        "gates": gates,
        "wh_words": wh_words,
        "wh_scales": wh_scales,
        "bh": bh,
        "wp_words": wp_words,
        "wp_scales": wp_scales,
        "g": g,
    }


def core(x, z, gates, wh_words, wh_scales, bh, wp_words, wp_scales, g):
    m = modulator(z, gates, wh_words, wh_scales, bh)
    p = mxq(f64(g), 1, "e4m3") @ unpack4(wp_words, wp_scales)
    s = p * m
    root_t = np.sqrt(x.shape[0])
    dwq = (mxq(f64(x), 0, "e4m3").T @ mxq(s, 0, "e4m3")) / root_t
    return dwq


def e4m3fn_bytes(y):
    return np.clip(np.asarray(y, np.float64), -448.0, 448.0).astype(np.float32).astype(ml_dtypes.float8_e4m3fn).view(np.uint8)


def e4m3fn_values(b):
    return np.asarray(b, np.uint8).view(ml_dtypes.float8_e4m3fn).astype(np.float64)


def setup_inputs():
    d = draw0()
    x0 = np.asarray(d['x']).astype(np.float64)
    s = (np.max(np.abs(x0), axis=(1,), keepdims=True) / 448.0).astype(np.float32)
    out = {}
    for k, v in d.items():
        if k == 'x':
            out['x_bytes'] = e4m3fn_bytes(x0 / s.astype(np.float64))
            out['x_scale'] = s
        else:
            out[k] = v
    return out


def reference(x_bytes, x_scale, z, gates, wh_words, wh_scales, bh, wp_words, wp_scales, g):
    return core(e4m3fn_values(x_bytes) * x_scale.astype(np.float64), z, gates, wh_words, wh_scales, bh, wp_words, wp_scales, g)

@@ -1,0 +1,353 @@
+from contextlib import ExitStack
+
+import concourse.mybir as mybir
+from concourse.masks import make_identity
+
+F32 = mybir.dt.float32
+BF16 = mybir.dt.bfloat16
+U32 = mybir.dt.uint32
+I32 = mybir.dt.int32
+U8 = mybir.dt.uint8
+FP8 = mybir.dt.float8_e4m3fn
+FP8X4 = mybir.dt.float8_e4m3fn_x4
+FP4X4 = mybir.dt.float4_e2m1fn_x4
+MULT = mybir.AluOpType.mult
+ADD = mybir.AluOpType.add
+COPY = mybir.ActivationFunctionType.Copy
+
+T = 1024
+D = 1024
+L = 3
+P = 128
+J = 4
+H = 2
+A = 2
+EB = 128
+NEB = D // EB
+
+FLOPS = 3 * 2 * T * D * D + 2 * L * T * D + 2 * T * D
+
+
+def tile_focalmodulationqueryweightgrad_w4_kernel(
+    tc, x_bytes, x_scale, z, gates, wh_words, wh_scales, bh, wp_words, wp_scales, g, out
+):
+    nc = tc.nc
+    with ExitStack() as ctx:
+        keep = ctx.enter_context(tc.tile_pool(name="keep", bufs=1))
+        work = ctx.enter_context(tc.tile_pool(name="work", bufs=2))
+        psum = ctx.enter_context(tc.psum_pool(name="psum", bufs=1))
+        ctx.enter_context(tc.manual_schedule())
+
+        gate_sb = keep.tile([P, H, J * L], BF16, name="gate_sb")
+        nc.scalar.dma_start(out=gate_sb[:], in_=gates.rearrange("(h m j) l -> m h (j l)", h=H, j=J))
+        xs_sb = keep.tile([P, H, J], F32, name="xs_sb")
+        nc.scalar.dma_start(out=xs_sb[:], in_=x_scale.rearrange("(h m j) o -> m h (j o)", h=H, j=J))
+
+        ident = keep.tile([P, P], F32, name="ident")
+        make_identity(nc, ident[:])
+        bh_row = keep.tile([P, D], BF16, name="bh_row")
+        nc.vector.memset(bh_row[:], 0.0)
+        w_sc = keep.tile([P, 4, D], U8, name="w_sc", align_bytes=64)
+        nc.vector.memset(w_sc[:].rearrange("p s n -> p (s n)").bitcast(I32), 0)
+        ident_bf = keep.tile([P, P], BF16, name="ident_bf")
+        nc.vector.tensor_copy(out=ident_bf[:], in_=ident[:])
+        nc.scalar.dma_start(out=bh_row[0:1, :], in_=bh.rearrange("(o n) -> o n", o=1))
+        ones = keep.tile([P, P], BF16, name="ones")
+        nc.vector.memset(ones[:], 1.0)
+
+        g_view = g.rearrange("(h m j) k -> h m (j k)", h=H, j=J)
+        z_view = z.rearrange("l (h m j) d -> h m l (j d)", h=H, j=J)
+        x_view = x_bytes.rearrange("(h m j) n -> h m (j n)", h=H, j=J)
+        g_sb = {}
+        z_sb = {}
+        x_sb = {}
+
+        def load_g(h):
+            for q in range(2):
+                t = keep.tile([P, 2, D], BF16, name=f"g_sb{h}{q}", align_bytes=64)
+                nc.sync.dma_start(out=t[:].rearrange("p j k -> p (j k)"), in_=g_view[h][:, 2048 * q : 2048 * (q + 1)])
+                g_sb[h, q] = t
+
+        def load_z(h, j):
+            t = keep.tile([P, L, D], BF16, name=f"z_sb{h}{j}", align_bytes=64)
+            nc.sync.dma_start(out=t[:], in_=z_view[h][:, :, D * j : D * (j + 1)])
+            z_sb[h, j] = t
+
+        def load_x(h):
+            t = keep.tile([P, J * D], U8, name=f"x_sb{h}", align_bytes=64)
+            nc.sync.dma_start(out=t[:], in_=x_view[h])
+            x_sb[h] = t
+
+        w_sb = {}
+
+        def load_w(key, words, scales, slot):
+            t = keep.tile([P, A, 2 * D], U8, name=f"w_{key}", align_bytes=64)
+            nc.sync.dma_start(out=t[:].bitcast(I32), in_=words.bitcast(I32).rearrange("a p n -> p a n"))
+            sv = scales.bitcast(I32).rearrange("a (q r) n -> r q a n", r=4)
+            for r in range(4):
+                nc.sync.dma_start(out=w_sc[r:P:32, slot : slot + A, :].bitcast(I32), in_=sv[r])
+            w_sb[key] = (t, slot)
+
+        for j in range(J):
+            load_z(0, j)
+        load_g(0)
+        load_w("h", wh_words, wh_scales, 2)
+        load_w("p", wp_words, wp_scales, 0)
+        load_x(0)
+        for j in range(J):
+            load_z(1, j)
+        load_g(1)
+        load_x(1)
+
+        def pe_levels(h, j):
+            return 3 if (h, j) in () else 2
+
+        diag = {}
+
+        def make_diag(h, j):
+            for l in range(pe_levels(h, j)):
+                t = keep.tile([P, P], BF16, name=f"diag{h}{j}{l}")
+                c = j * L + l
+                (nc.vector if (h, j) in ((0, 0), (0, 1), (0, 2), (0, 3)) else nc.gpsimd).tensor_scalar(
+                    out=t[:], in0=ident_bf[:], scalar1=gate_sb[:, h, c : c + 1], scalar2=0.0, op0=MULT, op1=ADD
+                )
+                diag[h, j, l] = t
+
+        for h in range(H):
+            for j in range(J):
+                make_diag(h, j)
+
+        bh_bc = keep.tile([P, D], F32, name="bh_bc")
+
+        def spread_bias():
+            for e in range(2):
+                b = psum.tile([P, 512], F32, name=f"bias{e}", tag="mp", bufs=4)
+                nc.tensor.matmul(b[:], lhsT=ones[:], rhs=bh_row[:, 512 * e : 512 * (e + 1)], start=True, stop=True)
+                nc.scalar.copy(out=bh_bc[:, 512 * e : 512 * (e + 1)], in_=b[:])
+
+        codes = {}
+        kin = {}
+        for key in ("g", "c"):
+            for h in range(H):
+                q = keep.tile([P, 2, A, 256], U32, name=f"{key}q{h}", align_bytes=64)
+                s = keep.tile([P, 2, A, 256], U8, name=f"{key}s{h}", align_bytes=64)
+                codes[key, h] = (q, s)
+        for key in ("x", "s"):
+            for h in range(H):
+                q = keep.tile([P, D], U32, name=f"{key}q{h}", align_bytes=64)
+                s = keep.tile([P, D], U8, name=f"{key}s{h}", align_bytes=64)
+                codes[key, h] = (q, s)
+
+        def transpose_tile(key, h, j, src):
+            if j % 2 == 0:
+                kin[key, h, j // 2] = work.tile([P, A, 256, 4], BF16, name=f"kin_{key}{h}{j}", tag="kin", bufs=3, align_bytes=64)
+            dst = kin[key, h, j // 2]
+            words = src.bitcast(F32)
+            bank = psum.tile([P, A, 2, P], F32, name=f"tp_{key}{h}{j}", tag="tp", bufs=2)
+            for a in range(A):
+                for u in range(2):
+                    nc.tensor.transpose(bank[:, a, u, :], words[:, 256 * a + u : 256 * (a + 1) : 2], ident[:])
+            jj = j % 2
+            nc.scalar.copy(
+                out=dst[:, :, P * jj : P * (jj + 1), :].bitcast(F32), in_=bank[:].rearrange("p a u m -> p a m u")
+            )
+
+        def quantise_k(key, h, q):
+            cq, cs = codes[key, h]
+            src = kin[key, h, q]
+            nc.vector.quantize_mx(
+                out=cq[:, q, :, :].rearrange("p a n -> p (a n)").bitcast(FP8X4),
+                scales=cs[:, q, :, :].rearrange("p a n -> p (a n)"),
+                in_=src[:].rearrange("p a n t -> p (a n t)"),
+            )
+
+        def g_tile(h, j):
+            transpose_tile("g", h, j, g_sb[h, j // 2][:, j % 2, :])
+
+        dg = {}
+        cw = {}
+
+        def c_levels01(h, j):
+            zt = z_sb[h, j]
+            for a in range(A):
+                b = psum.tile([P, 512], F32, name=f"dg{h}{j}{a}", tag="dg", bufs=2)
+                n = pe_levels(h, j)
+                for l in range(n):
+                    nc.tensor.matmul(
+                        b[:],
+                        lhsT=diag[h, j, l][:],
+                        rhs=zt[:, l, 512 * a : 512 * (a + 1)],
+                        start=(l == 0),
+                        stop=(l == n - 1),
+                    )
+                dg[h, j, a] = b
+
+        def c_level2(h, j):
+            zt = z_sb[h, j]
+            t = work.tile([P, D], BF16, name=f"cw{h}{j}", tag="cw", bufs=3)
+            c = j * L + 2
+            for a in range(A):
+                if pe_levels(h, j) == L:
+                    nc.scalar.copy(out=t[:, 512 * a : 512 * (a + 1)], in_=dg[h, j, a][:])
+                    continue
+                nc.vector.scalar_tensor_tensor(
+                    out=t[:, 512 * a : 512 * (a + 1)],
+                    in0=zt[:, 2, 512 * a : 512 * (a + 1)],
+                    scalar=gate_sb[:, h, c : c + 1],
+                    in1=dg[h, j, a][:],
+                    op0=MULT,
+                    op1=ADD,
+                )
+            cw[h, j] = t
+
+        def c_tile(h, j):
+            transpose_tile("c", h, j, cw[h, j][:])
+
+        mp = {}
+
+        def product(tag, key, wkey, h, e):
+            cq, cs = codes[key, h]
+            wt, slot = w_sb[wkey]
+            b = psum.tile([P, J, EB], F32, name=f"{wkey}_{h}{e}", tag="mp", bufs=4)
+            for j in range(J):
+                for a in range(A):
+                    nc.tensor.matmul_mx(
+                        b[:, j, :],
+                        lhsT=cq[:, j // 2, a, P * (j % 2) : P * (j % 2 + 1)].bitcast(FP8X4),
+                        lhsT_scale=cs[:, j // 2, a, P * (j % 2) : P * (j % 2 + 1)],
+                        rhs=wt[:, a, 2 * EB * e : 2 * EB * (e + 1)].bitcast(FP4X4),
+                        rhs_scale=w_sc[:, slot + a, EB * e : EB * (e + 1)],
+                        start=(a == 0),
+                        stop=(a == A - 1),
+                    )
+            mp[wkey, h, e] = b
+
+        mb = {}
+        sin = {}
+
+        def bias_m(h, e):
+            t = work.tile([P, EB, J], F32, name=f"mb{h}{e}", tag="mb", bufs=3)
+            nc.vector.tensor_tensor(
+                out=t[:],
+                in0=mp["h", h, e][:].rearrange("p j n -> p n j"),
+                in1=bh_bc[:, EB * e : EB * (e + 1)].unsqueeze(2).to_broadcast([P, EB, J]),
+                op=ADD,
+            )
+            mb[h, e] = t
+
+        def times_p(h, e):
+            if e % 2 == 0:
+                sin[h, e // 2] = work.tile([P, 2 * EB, J], BF16, name=f"sin{h}{e}", tag="sin", bufs=3, align_bytes=64)
+            t = sin[h, e // 2]
+            k = e % 2
+            nc.vector.tensor_tensor(
+                out=t[:, EB * k : EB * (k + 1), :],
+                in0=mp["p", h, e][:].rearrange("p j n -> p n j"),
+                in1=mb[h, e][:],
+                op=MULT,
+            )
+
+        def quantise_s(h, q):
+            sq, ss = codes["s", h]
+            nc.vector.quantize_mx(
+                out=sq[:, 256 * q : 256 * (q + 1)].bitcast(FP8X4),
+                scales=ss[:, 256 * q : 256 * (q + 1)],
+                in_=sin[h, q][:].rearrange("p n t -> p (n t)"),
+            )
+
+        xw = {}
+
+        def widen_x(h, j):
+            if j == 0:
+                xw[h] = work.tile([P, J, D], BF16, name=f"xw{h}", tag="xw", bufs=2)
+            nc.scalar.activation(
+                out=xw[h][:, j, :],
+                in_=x_sb[h][:, D * j : D * (j + 1)].bitcast(FP8),
+                func=COPY,
+                scale=xs_sb[:, h, j : j + 1],
+            )
+
+        xi = {}
+
+        def interleave_x(h, q):
+            t = work.tile([P, 512, J], BF16, name=f"xi{h}{q}", tag="xi", bufs=2, align_bytes=64)
+            src = xw[h][:, :, 512 * q : 512 * (q + 1)].rearrange("p j n -> p n j")
+            nc.scalar.copy(out=t[:], in_=src)
+            xi[h, q] = t
+
+        def quantise_x(h, q):
+            xq, xs = codes["x", h]
+            nc.vector.quantize_mx(
+                out=xq[:, 512 * q : 512 * (q + 1)].bitcast(FP8X4),
+                scales=xs[:, 512 * q : 512 * (q + 1)],
+                in_=xi[h, q][:].rearrange("p n t -> p (n t)"),
+            )
+
+        def out_tile(e, r, tag, bufs, engine):
+            b = psum.tile([P, 512], F32, name=f"o{e}{r}", tag=tag, bufs=bufs)
+            for h in range(H):
+                xq, xs = codes["x", h]
+                sq, ss = codes["s", h]
+                nc.tensor.matmul_mx(
+                    b[:],
+                    lhsT=xq[:, P * r : P * (r + 1)].bitcast(FP8X4),
+                    lhsT_scale=xs[:, P * r : P * (r + 1)],
+                    rhs=sq[:, 512 * e : 512 * (e + 1)].bitcast(FP8X4),
+                    rhs_scale=ss[:, 512 * e : 512 * (e + 1)],
+                    start=(h == 0),
+                    stop=(h == H - 1),
+                )
+            t = work.tile([P, 512], F32, name=f"ob{e}{r}", tag="ob", bufs=12)
+            if engine == 0:
+                nc.scalar.activation(out=t[:], in_=b[:], func=COPY, scale=1.0 / 32.0)
+            else:
+                nc.vector.tensor_scalar(out=t[:], in0=b[:], scalar1=1.0 / 32.0, scalar2=None, op0=MULT)
+            nc.sync.dma_start(out=out[P * r : P * (r + 1), 512 * e : 512 * (e + 1)], in_=t[:])
+
+        for j in range(J):
+            c_levels01(0, j)
+            if j > 0:
+                c_tile(0, j - 1)
+            c_level2(0, j)
+            if j == 2:
+                quantise_k("c", 0, 0)
+        g_tile(0, 0)
+        c_tile(0, 3)
+        g_tile(0, 1)
+        quantise_k("c", 0, 1)
+        quantise_k("g", 0, 0)
+        spread_bias()
+        g_tile(0, 2)
+        g_tile(0, 3)
+        quantise_k("g", 0, 1)
+
+        steps = [
+            lambda: (widen_x(0, 0), widen_x(0, 1)),
+            lambda: (widen_x(0, 2), widen_x(0, 3), c_levels01(1, 0)),
+            lambda: (c_level2(1, 0), interleave_x(0, 0), c_levels01(1, 1)),
+            lambda: (c_tile(1, 0), c_level2(1, 1), c_levels01(1, 2), interleave_x(0, 1), quantise_x(0, 0)),
+            lambda: (c_tile(1, 1), c_level2(1, 2), c_levels01(1, 3)),
+            lambda: (c_tile(1, 2), c_level2(1, 3), quantise_k("c", 1, 0), g_tile(1, 0), quantise_x(0, 1)),
+            lambda: (c_tile(1, 3), g_tile(1, 1), g_tile(1, 2), quantise_k("g", 1, 0), quantise_k("c", 1, 1)),
+            lambda: (g_tile(1, 3), widen_x(1, 0), widen_x(1, 1), quantise_k("g", 1, 1)),
+        ]
+        for i in range(H * NEB):
+            h, e = i // NEB, i % NEB
+            product("m", "c", "h", h, e)
+            bias_m(h, e)
+            product("p", "g", "p", h, e)
+            if h == 0:
+                steps[e]()
+            times_p(h, e)
+            if e % 2 == 1:
+                quantise_s(h, e // 2)
+            if h == 1 and e in (0, 1):
+                widen_x(1, e + 2)
+            if h == 1 and e in (2, 3):
+                interleave_x(1, e - 2)
+            if h == 1 and e in (4, 5):
+                quantise_x(1, e - 4)
+        for r in range(8):
+            out_tile(0, r, "tp" if r % 2 else "dg", 2, 0)
+        for r in range(8):
+            out_tile(1, r, "mp", 4, r % 2 if r >= 6 else 0)

@@ -36,7 +36,6 @@ def tile_focalmodulationqueryweightgrad_w4_kernel(
         keep = ctx.enter_context(tc.tile_pool(name="keep", bufs=1))
         work = ctx.enter_context(tc.tile_pool(name="work", bufs=2))
         psum = ctx.enter_context(tc.psum_pool(name="psum", bufs=1))
-        ctx.enter_context(tc.manual_schedule())
 
         gate_sb = keep.tile([P, H, J * L], BF16, name="gate_sb")
         nc.scalar.dma_start(out=gate_sb[:], in_=gates.rearrange("(h m j) l -> m h (j l)", h=H, j=J))
@@ -51,7 +50,10 @@ def tile_focalmodulationqueryweightgrad_w4_kernel(
         nc.vector.memset(w_sc[:].rearrange("p s n -> p (s n)").bitcast(I32), 0)
         ident_bf = keep.tile([P, P], BF16, name="ident_bf")
         nc.vector.tensor_copy(out=ident_bf[:], in_=ident[:])
-        nc.scalar.dma_start(out=bh_row[0:1, :], in_=bh.rearrange("(o n) -> o n", o=1))
+
+        def load_bias():
+            nc.sync.dma_start(out=bh_row[0:1, :], in_=bh.rearrange("(o n) -> o n", o=1))
+
         ones = keep.tile([P, P], BF16, name="ones")
         nc.vector.memset(ones[:], 1.0)
 
@@ -90,8 +92,9 @@ def tile_focalmodulationqueryweightgrad_w4_kernel(
 
         for j in range(J):
             load_z(0, j)
-        load_g(0)
         load_w("h", wh_words, wh_scales, 2)
+        load_bias()
+        load_g(0)
         load_w("p", wp_words, wp_scales, 0)
         load_x(0)
         for j in range(J):
@@ -146,7 +149,11 @@ def tile_focalmodulationqueryweightgrad_w4_kernel(
             bank = psum.tile([P, A, 2, P], F32, name=f"tp_{key}{h}{j}", tag="tp", bufs=2)
             for a in range(A):
                 for u in range(2):
-                    nc.tensor.transpose(bank[:, a, u, :], words[:, 256 * a + u : 256 * (a + 1) : 2], ident[:])
+                    if key == "c":
+                        cols = words[:, 256 * a + P * u : 256 * a + P * (u + 1)]
+                    else:
+                        cols = words[:, 256 * a + u : 256 * (a + 1) : 2]
+                    nc.tensor.transpose(bank[:, a, u, :], cols, ident[:])
             jj = j % 2
             nc.scalar.copy(
                 out=dst[:, :, P * jj : P * (jj + 1), :].bitcast(F32), in_=bank[:].rearrange("p a u m -> p a m u")
@@ -190,14 +197,15 @@ def tile_focalmodulationqueryweightgrad_w4_kernel(
                 if pe_levels(h, j) == L:
                     nc.scalar.copy(out=t[:, 512 * a : 512 * (a + 1)], in_=dg[h, j, a][:])
                     continue
-                nc.vector.scalar_tensor_tensor(
-                    out=t[:, 512 * a : 512 * (a + 1)],
-                    in0=zt[:, 2, 512 * a : 512 * (a + 1)],
-                    scalar=gate_sb[:, h, c : c + 1],
-                    in1=dg[h, j, a][:],
-                    op0=MULT,
-                    op1=ADD,
-                )
+                for u in range(2):
+                    nc.vector.scalar_tensor_tensor(
+                        out=t[:, 512 * a + 256 * u : 512 * a + 256 * (u + 1)].rearrange("p (k e) -> p k e", e=2),
+                        in0=zt[:, 2, 512 * a : 512 * (a + 1)].rearrange("p (k u e) -> p u k e", u=2, e=2)[:, u],
+                        scalar=gate_sb[:, h, c : c + 1],
+                        in1=dg[h, j, a][:].rearrange("p (k u e) -> p u k e", u=2, e=2)[:, u],
+                        op0=MULT,
+                        op1=ADD,
+                    )
             cw[h, j] = t
 
         def c_tile(h, j):
@@ -315,10 +323,12 @@ def tile_focalmodulationqueryweightgrad_w4_kernel(
         c_tile(0, 3)
         g_tile(0, 1)
         quantise_k("c", 0, 1)
-        quantise_k("g", 0, 0)
         spread_bias()
+        quantise_k("g", 0, 0)
         g_tile(0, 2)
         g_tile(0, 3)
+        product("m", "c", "h", 0, 0)
+        bias_m(0, 0)
         quantise_k("g", 0, 1)
 
         steps = [
@@ -333,11 +343,13 @@ def tile_focalmodulationqueryweightgrad_w4_kernel(
         ]
         for i in range(H * NEB):
             h, e = i // NEB, i % NEB
-            product("m", "c", "h", h, e)
-            bias_m(h, e)
+            if i + 1 < H * NEB:
+                product("m", "c", "h", (i + 1) // NEB, (i + 1) % NEB)
             product("p", "g", "p", h, e)
             if h == 0:
                 steps[e]()
+            if i + 1 < H * NEB:
+                bias_m((i + 1) // NEB, (i + 1) % NEB)
             times_p(h, e)
             if e % 2 == 1:
                 quantise_s(h, e // 2)

from contextlib import ExitStack

import concourse.mybir as mybir
from concourse.masks import make_identity

F32 = mybir.dt.float32
BF16 = mybir.dt.bfloat16
U32 = mybir.dt.uint32
I32 = mybir.dt.int32
U8 = mybir.dt.uint8
FP8 = mybir.dt.float8_e4m3fn
FP8X4 = mybir.dt.float8_e4m3fn_x4
FP4X4 = mybir.dt.float4_e2m1fn_x4
MULT = mybir.AluOpType.mult
ADD = mybir.AluOpType.add
COPY = mybir.ActivationFunctionType.Copy

T = 1024
D = 1024
L = 3
P = 128
J = 4
H = 2
A = 2
EB = 128
NEB = D // EB

FLOPS = 3 * 2 * T * D * D + 2 * L * T * D + 2 * T * D


def tile_focalmodulationqueryweightgrad_w4_kernel(
    tc, x_bytes, x_scale, z, gates, wh_words, wh_scales, bh, wp_words, wp_scales, g, out
):
    nc = tc.nc
    with ExitStack() as ctx:
        keep = ctx.enter_context(tc.tile_pool(name="keep", bufs=1))
        work = ctx.enter_context(tc.tile_pool(name="work", bufs=2))
        psum = ctx.enter_context(tc.psum_pool(name="psum", bufs=1))

        gate_sb = keep.tile([P, H, J * L], BF16, name="gate_sb")
        nc.scalar.dma_start(out=gate_sb[:], in_=gates.rearrange("(h m j) l -> m h (j l)", h=H, j=J))
        xs_sb = keep.tile([P, H, J], F32, name="xs_sb")
        nc.scalar.dma_start(out=xs_sb[:], in_=x_scale.rearrange("(h m j) o -> m h (j o)", h=H, j=J))

        ident = keep.tile([P, P], F32, name="ident")
        make_identity(nc, ident[:])
        bh_row = keep.tile([P, D], BF16, name="bh_row")
        nc.vector.memset(bh_row[:], 0.0)
        w_sc = keep.tile([P, 4, D], U8, name="w_sc", align_bytes=64)
        nc.vector.memset(w_sc[:].rearrange("p s n -> p (s n)").bitcast(I32), 0)
        ident_bf = keep.tile([P, P], BF16, name="ident_bf")
        nc.vector.tensor_copy(out=ident_bf[:], in_=ident[:])

        def load_bias():
            nc.sync.dma_start(out=bh_row[0:1, :], in_=bh.rearrange("(o n) -> o n", o=1))

        ones = keep.tile([P, P], BF16, name="ones")
        nc.vector.memset(ones[:], 1.0)

        g_view = g.rearrange("(h m j) k -> h m (j k)", h=H, j=J)
        z_view = z.rearrange("l (h m j) d -> h m l (j d)", h=H, j=J)
        x_view = x_bytes.rearrange("(h m j) n -> h m (j n)", h=H, j=J)
        g_sb = {}
        z_sb = {}
        x_sb = {}

        def load_g(h):
            for q in range(2):
                t = keep.tile([P, 2, D], BF16, name=f"g_sb{h}{q}", align_bytes=64)
                nc.sync.dma_start(out=t[:].rearrange("p j k -> p (j k)"), in_=g_view[h][:, 2048 * q : 2048 * (q + 1)])
                g_sb[h, q] = t

        def load_z(h, j):
            t = keep.tile([P, L, D], BF16, name=f"z_sb{h}{j}", align_bytes=64)
            nc.sync.dma_start(out=t[:], in_=z_view[h][:, :, D * j : D * (j + 1)])
            z_sb[h, j] = t

        def load_x(h):
            t = keep.tile([P, J * D], U8, name=f"x_sb{h}", align_bytes=64)
            nc.sync.dma_start(out=t[:], in_=x_view[h])
            x_sb[h] = t

        w_sb = {}

        def load_w(key, words, scales, slot):
            t = keep.tile([P, A, 2 * D], U8, name=f"w_{key}", align_bytes=64)
            nc.sync.dma_start(out=t[:].bitcast(I32), in_=words.bitcast(I32).rearrange("a p n -> p a n"))
            sv = scales.bitcast(I32).rearrange("a (q r) n -> r q a n", r=4)
            for r in range(4):
                nc.sync.dma_start(out=w_sc[r:P:32, slot : slot + A, :].bitcast(I32), in_=sv[r])
            w_sb[key] = (t, slot)

        for j in range(J):
            load_z(0, j)
        load_w("h", wh_words, wh_scales, 2)
        load_bias()
        load_g(0)
        load_w("p", wp_words, wp_scales, 0)
        load_x(0)
        for j in range(J):
            load_z(1, j)
        load_g(1)
        load_x(1)

        def pe_levels(h, j):
            return 3 if (h, j) in () else 2

        diag = {}

        def make_diag(h, j):
            for l in range(pe_levels(h, j)):
                t = keep.tile([P, P], BF16, name=f"diag{h}{j}{l}")
                c = j * L + l
                (nc.vector if (h, j) in ((0, 0), (0, 1), (0, 2), (0, 3)) else nc.gpsimd).tensor_scalar(
                    out=t[:], in0=ident_bf[:], scalar1=gate_sb[:, h, c : c + 1], scalar2=0.0, op0=MULT, op1=ADD
                )
                diag[h, j, l] = t

        for h in range(H):
            for j in range(J):
                make_diag(h, j)

        bh_bc = keep.tile([P, D], F32, name="bh_bc")

        def spread_bias():
            for e in range(2):
                b = psum.tile([P, 512], F32, name=f"bias{e}", tag="mp", bufs=4)
                nc.tensor.matmul(b[:], lhsT=ones[:], rhs=bh_row[:, 512 * e : 512 * (e + 1)], start=True, stop=True)
                nc.scalar.copy(out=bh_bc[:, 512 * e : 512 * (e + 1)], in_=b[:])

        codes = {}
        kin = {}
        for key in ("g", "c"):
            for h in range(H):
                q = keep.tile([P, 2, A, 256], U32, name=f"{key}q{h}", align_bytes=64)
                s = keep.tile([P, 2, A, 256], U8, name=f"{key}s{h}", align_bytes=64)
                codes[key, h] = (q, s)
        for key in ("x", "s"):
            for h in range(H):
                q = keep.tile([P, D], U32, name=f"{key}q{h}", align_bytes=64)
                s = keep.tile([P, D], U8, name=f"{key}s{h}", align_bytes=64)
                codes[key, h] = (q, s)

        def transpose_tile(key, h, j, src):
            if j % 2 == 0:
                kin[key, h, j // 2] = work.tile([P, A, 256, 4], BF16, name=f"kin_{key}{h}{j}", tag="kin", bufs=3, align_bytes=64)
            dst = kin[key, h, j // 2]
            words = src.bitcast(F32)
            bank = psum.tile([P, A, 2, P], F32, name=f"tp_{key}{h}{j}", tag="tp", bufs=2)
            for a in range(A):
                for u in range(2):
                    if key == "c":
                        cols = words[:, 256 * a + P * u : 256 * a + P * (u + 1)]
                    else:
                        cols = words[:, 256 * a + u : 256 * (a + 1) : 2]
                    nc.tensor.transpose(bank[:, a, u, :], cols, ident[:])
            jj = j % 2
            nc.scalar.copy(
                out=dst[:, :, P * jj : P * (jj + 1), :].bitcast(F32), in_=bank[:].rearrange("p a u m -> p a m u")
            )

        def quantise_k(key, h, q):
            cq, cs = codes[key, h]
            src = kin[key, h, q]
            nc.vector.quantize_mx(
                out=cq[:, q, :, :].rearrange("p a n -> p (a n)").bitcast(FP8X4),
                scales=cs[:, q, :, :].rearrange("p a n -> p (a n)"),
                in_=src[:].rearrange("p a n t -> p (a n t)"),
            )

        def g_tile(h, j):
            transpose_tile("g", h, j, g_sb[h, j // 2][:, j % 2, :])

        dg = {}
        cw = {}

        def c_levels01(h, j):
            zt = z_sb[h, j]
            for a in range(A):
                b = psum.tile([P, 512], F32, name=f"dg{h}{j}{a}", tag="dg", bufs=2)
                n = pe_levels(h, j)
                for l in range(n):
                    nc.tensor.matmul(
                        b[:],
                        lhsT=diag[h, j, l][:],
                        rhs=zt[:, l, 512 * a : 512 * (a + 1)],
                        start=(l == 0),
                        stop=(l == n - 1),
                    )
                dg[h, j, a] = b

        def c_level2(h, j):
            zt = z_sb[h, j]
            t = work.tile([P, D], BF16, name=f"cw{h}{j}", tag="cw", bufs=3)
            c = j * L + 2
            for a in range(A):
                if pe_levels(h, j) == L:
                    nc.scalar.copy(out=t[:, 512 * a : 512 * (a + 1)], in_=dg[h, j, a][:])
                    continue
                for u in range(2):
                    nc.vector.scalar_tensor_tensor(
                        out=t[:, 512 * a + 256 * u : 512 * a + 256 * (u + 1)].rearrange("p (k e) -> p k e", e=2),
                        in0=zt[:, 2, 512 * a : 512 * (a + 1)].rearrange("p (k u e) -> p u k e", u=2, e=2)[:, u],
                        scalar=gate_sb[:, h, c : c + 1],
                        in1=dg[h, j, a][:].rearrange("p (k u e) -> p u k e", u=2, e=2)[:, u],
                        op0=MULT,
                        op1=ADD,
                    )
            cw[h, j] = t

        def c_tile(h, j):
            transpose_tile("c", h, j, cw[h, j][:])

        mp = {}

        def product(tag, key, wkey, h, e):
            cq, cs = codes[key, h]
            wt, slot = w_sb[wkey]
            b = psum.tile([P, J, EB], F32, name=f"{wkey}_{h}{e}", tag="mp", bufs=4)
            for j in range(J):
                for a in range(A):
                    nc.tensor.matmul_mx(
                        b[:, j, :],
                        lhsT=cq[:, j // 2, a, P * (j % 2) : P * (j % 2 + 1)].bitcast(FP8X4),
                        lhsT_scale=cs[:, j // 2, a, P * (j % 2) : P * (j % 2 + 1)],
                        rhs=wt[:, a, 2 * EB * e : 2 * EB * (e + 1)].bitcast(FP4X4),
                        rhs_scale=w_sc[:, slot + a, EB * e : EB * (e + 1)],
                        start=(a == 0),
                        stop=(a == A - 1),
                    )
            mp[wkey, h, e] = b

        mb = {}
        sin = {}

        def bias_m(h, e):
            t = work.tile([P, EB, J], F32, name=f"mb{h}{e}", tag="mb", bufs=3)
            nc.vector.tensor_tensor(
                out=t[:],
                in0=mp["h", h, e][:].rearrange("p j n -> p n j"),
                in1=bh_bc[:, EB * e : EB * (e + 1)].unsqueeze(2).to_broadcast([P, EB, J]),
                op=ADD,
            )
            mb[h, e] = t

        def times_p(h, e):
            if e % 2 == 0:
                sin[h, e // 2] = work.tile([P, 2 * EB, J], BF16, name=f"sin{h}{e}", tag="sin", bufs=3, align_bytes=64)
            t = sin[h, e // 2]
            k = e % 2
            nc.vector.tensor_tensor(
                out=t[:, EB * k : EB * (k + 1), :],
                in0=mp["p", h, e][:].rearrange("p j n -> p n j"),
                in1=mb[h, e][:],
                op=MULT,
            )

        def quantise_s(h, q):
            sq, ss = codes["s", h]
            nc.vector.quantize_mx(
                out=sq[:, 256 * q : 256 * (q + 1)].bitcast(FP8X4),
                scales=ss[:, 256 * q : 256 * (q + 1)],
                in_=sin[h, q][:].rearrange("p n t -> p (n t)"),
            )

        xw = {}

        def widen_x(h, j):
            if j == 0:
                xw[h] = work.tile([P, J, D], BF16, name=f"xw{h}", tag="xw", bufs=2)
            nc.scalar.activation(
                out=xw[h][:, j, :],
                in_=x_sb[h][:, D * j : D * (j + 1)].bitcast(FP8),
                func=COPY,
                scale=xs_sb[:, h, j : j + 1],
            )

        xi = {}

        def interleave_x(h, q):
            t = work.tile([P, 512, J], BF16, name=f"xi{h}{q}", tag="xi", bufs=2, align_bytes=64)
            src = xw[h][:, :, 512 * q : 512 * (q + 1)].rearrange("p j n -> p n j")
            nc.scalar.copy(out=t[:], in_=src)
            xi[h, q] = t

        def quantise_x(h, q):
            xq, xs = codes["x", h]
            nc.vector.quantize_mx(
                out=xq[:, 512 * q : 512 * (q + 1)].bitcast(FP8X4),
                scales=xs[:, 512 * q : 512 * (q + 1)],
                in_=xi[h, q][:].rearrange("p n t -> p (n t)"),
            )

        def out_tile(e, r, tag, bufs, engine):
            b = psum.tile([P, 512], F32, name=f"o{e}{r}", tag=tag, bufs=bufs)
            for h in range(H):
                xq, xs = codes["x", h]
                sq, ss = codes["s", h]
                nc.tensor.matmul_mx(
                    b[:],
                    lhsT=xq[:, P * r : P * (r + 1)].bitcast(FP8X4),
                    lhsT_scale=xs[:, P * r : P * (r + 1)],
                    rhs=sq[:, 512 * e : 512 * (e + 1)].bitcast(FP8X4),
                    rhs_scale=ss[:, 512 * e : 512 * (e + 1)],
                    start=(h == 0),
                    stop=(h == H - 1),
                )
            t = work.tile([P, 512], F32, name=f"ob{e}{r}", tag="ob", bufs=12)
            if engine == 0:
                nc.scalar.activation(out=t[:], in_=b[:], func=COPY, scale=1.0 / 32.0)
            else:
                nc.vector.tensor_scalar(out=t[:], in0=b[:], scalar1=1.0 / 32.0, scalar2=None, op0=MULT)
            nc.sync.dma_start(out=out[P * r : P * (r + 1), 512 * e : 512 * (e + 1)], in_=t[:])

        for j in range(J):
            c_levels01(0, j)
            if j > 0:
                c_tile(0, j - 1)
            c_level2(0, j)
            if j == 2:
                quantise_k("c", 0, 0)
        g_tile(0, 0)
        c_tile(0, 3)
        g_tile(0, 1)
        quantise_k("c", 0, 1)
        spread_bias()
        quantise_k("g", 0, 0)
        g_tile(0, 2)
        g_tile(0, 3)
        product("m", "c", "h", 0, 0)
        bias_m(0, 0)
        quantise_k("g", 0, 1)

        steps = [
            lambda: (widen_x(0, 0), widen_x(0, 1)),
            lambda: (widen_x(0, 2), widen_x(0, 3), c_levels01(1, 0)),
            lambda: (c_level2(1, 0), interleave_x(0, 0), c_levels01(1, 1)),
            lambda: (c_tile(1, 0), c_level2(1, 1), c_levels01(1, 2), interleave_x(0, 1), quantise_x(0, 0)),
            lambda: (c_tile(1, 1), c_level2(1, 2), c_levels01(1, 3)),
            lambda: (c_tile(1, 2), c_level2(1, 3), quantise_k("c", 1, 0), g_tile(1, 0), quantise_x(0, 1)),
            lambda: (c_tile(1, 3), g_tile(1, 1), g_tile(1, 2), quantise_k("g", 1, 0), quantise_k("c", 1, 1)),
            lambda: (g_tile(1, 3), widen_x(1, 0), widen_x(1, 1), quantise_k("g", 1, 1)),
        ]
        for i in range(H * NEB):
            h, e = i // NEB, i % NEB
            if i + 1 < H * NEB:
                product("m", "c", "h", (i + 1) // NEB, (i + 1) % NEB)
            product("p", "g", "p", h, e)
            if h == 0:
                steps[e]()
            if i + 1 < H * NEB:
                bias_m((i + 1) // NEB, (i + 1) % NEB)
            times_p(h, e)
            if e % 2 == 1:
                quantise_s(h, e // 2)
            if h == 1 and e in (0, 1):
                widen_x(1, e + 2)
            if h == 1 and e in (2, 3):
                interleave_x(1, e - 2)
            if h == 1 and e in (4, 5):
                quantise_x(1, e - 4)
        for r in range(8):
            out_tile(0, r, "tp" if r % 2 else "dg", 2, 0)
        for r in range(8):
            out_tile(1, r, "mp", 4, r % 2 if r >= 6 else 0)
